import numpy as np
import ml_dtypes


def mxq(x, axis, fmt="e4m3"):
    dtype, down = {"e4m3": (ml_dtypes.float8_e4m3fn, 7), "e5m2": (ml_dtypes.float8_e5m2, 14)}[fmt]
    v = np.moveaxis(np.asarray(x, np.float32).astype(ml_dtypes.bfloat16).astype(np.float64), axis, -1)
    blocks = v.reshape(v.shape[:-1] + (-1, 32))
    amax = np.abs(blocks).max(-1, keepdims=True)
    byte = np.maximum(np.where(amax > 0, np.frexp(amax)[1] - 1 + 127, 0) - down, 1)
    scale = np.exp2(byte - 127.0)
    codes = (blocks / scale).astype(np.float32).astype(dtype).astype(np.float64)
    return np.moveaxis((codes * scale).reshape(v.shape), -1, axis)


WIDE = False


def mx_kscale(k):
    if not WIDE:
        return np.ones(k)
    levels = np.array([10, -10, 5, -5, 0])
    if k % 512:
        return np.exp2(np.random.permutation(np.resize(levels, k // 32))).repeat(32)
    a = np.empty((k // 512, 16))
    for p in range(k // 512):
        a[p, :8] = np.random.permutation(np.resize(levels, 8))
        for g in range(8):
            far = levels[np.abs(levels - a[p, g]) >= 10]
            a[p, g + 8] = far[np.random.randint(len(far))]
    return np.exp2(a.ravel()).repeat(32)


def f64(x):
    return np.asarray(x).astype(np.float64)


def striped(idx):
    return np.tile(idx.reshape(-1, 16).T, (8, 1)).astype(np.uint16)


def unstriped(offs):
    return offs[:16].T.reshape(-1).astype(np.int64)


def pack_weight(w):
    k, n = w.shape
    w = f64(np.asarray(w, np.float32).astype(ml_dtypes.bfloat16)).reshape(k // 32, 32, n)
    amax = np.abs(w).max(1)
    byte = np.clip(np.where(amax > 0, np.frexp(amax)[1] - 1 + 127 - 7, 1), 1, 254)
    scaled = (w * np.exp2(127.0 - byte)[:, None, :]).reshape(k, n).astype(np.float32)
    words = np.ascontiguousarray(scaled.reshape(k // 512, 128, 4, n).transpose(0, 1, 3, 2)).astype(ml_dtypes.float8_e4m3fn).view(np.uint8)
    return words, np.ascontiguousarray(byte.astype(np.uint8).reshape(k // 512, 16, n))


def unpack_weight(words, scales):
    g, p, n, _ = words.shape
    vals = np.ascontiguousarray(words).view(ml_dtypes.float8_e4m3fn).astype(np.float64) * np.repeat(np.exp2(scales.astype(np.float64) - 127.0), 8, axis=1)[..., None]
    return vals.transpose(0, 1, 3, 2).reshape(g * 512, n)


def silu(v):
    return v / (1.0 + np.exp(-np.maximum(v, -700.0)))


K, T, S, N, H = 512, 2048, 512, 512, 512


def setup_inputs():
    n = np.random.standard_normal
    s = mx_kscale(K)[:, None]
    u = mx_kscale(S)
    packed_xT = pack_weight(n((K, T)) * s)
    return {
        "x_words": packed_xT[0],
        "x_scales": packed_xT[1],
        "wa": (n((K, H)) / np.sqrt(K) / s).astype(np.float32),
        "wb": (n((K, H)) / np.sqrt(K) / s).astype(np.float32),
        "gt": (np.random.uniform(0.5, 1.5, (S, 1)) * u[:, None]).astype(np.float32),
        "reg": n((N, H)).astype(np.float32),
        "w1": (n((S, N)) / np.sqrt(S) / u[:, None]).astype(np.float32),
        "offs": striped(np.random.permutation(T)[:S]),
    }


def reference(x_words, x_scales, wa, wb, gt, reg, w1, offs):
    xq = unpack_weight(x_words, x_scales)[:, unstriped(offs)]
    a = xq.T @ mxq(f64(wa), 0, "e4m3")
    b = xq.T @ mxq(f64(wb), 0, "e4m3")
    z = f64(gt) * (silu(a) * b)
    return f64(reg) + (mxq(f64(w1), 0, "e4m3").T @ mxq(z, 0, "e4m3"))

@@ -1,0 +1,217 @@
+from contextlib import ExitStack
+
+import concourse.mybir as mybir
+
+K, T, S, N, H = 512, 2048, 512, 512, 512
+FLOPS = 2 * K * S * H * 2 + 2 * S * N * H
+
+F32 = mybir.dt.float32
+BF16 = mybir.dt.bfloat16
+I32 = mybir.dt.int32
+U32 = mybir.dt.uint32
+U16 = mybir.dt.uint16
+U8 = mybir.dt.uint8
+FP8X4 = mybir.dt.float8_e4m3fn_x4
+MULT = mybir.AluOpType.mult
+ADD = mybir.AluOpType.add
+SILU = mybir.ActivationFunctionType.Silu
+
+P = 128
+PACK = 4
+HALF = 256
+
+
+def interleave(nc, engine, dst, src):
+    dst_walk = dst.rearrange("p (c i) t -> p c t i", i=4)
+    src_walk = src.rearrange("p t (c i) -> p c t i", i=4)
+    if engine == "vector":
+        nc.vector.tensor_copy(out=dst_walk, in_=src_walk)
+    else:
+        nc.scalar.copy(out=dst_walk, in_=src_walk)
+
+
+def tile_picked_regmix_silu_p_kernel(
+    tc, x_words, x_scales, wa, wb, gt, reg, w1, offs, out
+):
+    nc = tc.nc
+    with ExitStack() as ctx:
+        keep = ctx.enter_context(tc.tile_pool(name="keep", bufs=1))
+        psum = ctx.enter_context(tc.psum_pool(name="psum", bufs=1))
+
+        offsets = keep.tile([P, S // 16], U16, name="offsets")
+        words = keep.tile([P, T], I32, name="words", align_bytes=64)
+        scale_rows = keep.tile([P, T], U8, name="scale_rows", align_bytes=64)
+        gate = keep.tile([P, PACK], F32, name="gate")
+        zero = keep.tile([P, 1], F32, name="zero")
+        zero_bias = keep.tile([P, 1], F32, name="zero_bias")
+
+        raw = {}
+
+        def load_half(name, src, h):
+            raw[name, h] = keep.tile([P, PACK, HALF], F32, name="raw_%s%d" % (name, h))
+            cols = slice(h * HALF, (h + 1) * HALF)
+            nc.sync.dma_start(out=raw[name, h][:], in_=src[:, cols].rearrange("(p t) c -> p t c", t=PACK))
+
+        def load_scales():
+            for q in range(4):
+                nc.sync.dma_start(
+                    out=scale_rows[32 * q : 32 * q + 4, :].bitcast(I32),
+                    in_=x_scales[0, 4 * q : 4 * q + 4, :].bitcast(I32),
+                )
+
+        def load_words():
+            nc.sync.dma_start(out=words[:], in_=x_words[0].rearrange("p n t -> p (n t)").bitcast(I32))
+
+        regs = {}
+
+        def load_reg(mp):
+            regs[mp] = keep.tile([P, 2, H], F32, name="reg%d" % mp)
+            rows = slice(mp * 2 * P, (mp + 1) * 2 * P)
+            nc.sync.dma_start(out=regs[mp][:], in_=reg[rows, :].rearrange("(q p) j -> p q j", p=P))
+
+        grouped = {}
+        codes = {}
+        scales = {}
+
+        def cast(name, h, engine):
+            grouped[name, h] = keep.tile([P, HALF, PACK], BF16, name="grouped_%s%d" % (name, h), align_bytes=64)
+            interleave(nc, engine, grouped[name, h][:], raw[name, h][:])
+
+        def quantize(name, h):
+            codes[name, h] = keep.tile([P, HALF], U32, name="codes_%s%d" % (name, h), align_bytes=64)
+            scales[name, h] = keep.tile([P, HALF], U8, name="scales_%s%d" % (name, h), align_bytes=64)
+            nc.vector.quantize_mx(
+                out=codes[name, h][:].bitcast(FP8X4),
+                scales=scales[name, h][:],
+                in_=grouped[name, h][:].rearrange("p c t -> p (c t)"),
+            )
+
+        x_codes = keep.tile([P, S], U32, name="x_codes", align_bytes=64)
+        x_bytes_listed = keep.tile([P, S], U8, name="x_bytes_listed", align_bytes=64)
+        x_bytes = keep.tile([P, S], U8, name="x_bytes", align_bytes=64)
+
+        def gather_scales():
+            nc.vector.tensor_copy(out=x_bytes_listed[:], in_=scale_rows[:].indirect(offsets[:]))
+
+        def deal_scales():
+            nc.vector.tensor_copy(
+                out=x_bytes[:].rearrange("p (t m) -> p t m", t=PACK),
+                in_=x_bytes_listed[:].rearrange("p (m t) -> p t m", t=PACK),
+            )
+
+        def gather_words():
+            nc.vector.tensor_copy(
+                out=x_codes[:].rearrange("p (t m) -> p m t", t=PACK),
+                in_=words[:].bitcast(U32).indirect(offsets[:]),
+            )
+
+        banks = {}
+
+        def first_product(name, h):
+            for tp in range(2):
+                tag = "%s%d%d" % (name, h, tp)
+                banks[name, h, tp] = psum.tile([P, 2, HALF], F32, name="bank_" + tag, tag=tag)
+                for e in range(2):
+                    cols = slice((2 * tp + e) * P, (2 * tp + e + 1) * P)
+                    nc.tensor.matmul_mx(
+                        out=banks[name, h, tp][:, e, :],
+                        lhsT=x_codes[:, cols].bitcast(FP8X4),
+                        lhsT_scale=x_bytes[:, cols],
+                        rhs=codes[name, h][:].bitcast(FP8X4),
+                        rhs_scale=scales[name, h][:],
+                        start=True,
+                        stop=True,
+                    )
+
+        silus = {}
+
+        def silu(h):
+            for tp in range(2):
+                silus[h, tp] = keep.tile([P, 2, HALF], F32, name="silu%d%d" % (h, tp))
+                nc.scalar.activation(out=silus[h, tp][:], in_=banks["wa", h, tp][:], func=SILU, bias=zero_bias[:])
+
+        def gated(h):
+            raw["z", h] = keep.tile([P, PACK, HALF], BF16, name="raw_z%d" % h)
+            for t in range(PACK):
+                nc.vector.scalar_tensor_tensor(
+                    out=raw["z", h][:, t, :],
+                    in0=banks["wb", h, t // 2][:, t % 2, :],
+                    scalar=gate[:, t : t + 1],
+                    in1=silus[h, t // 2][:, t % 2, :],
+                    op0=MULT,
+                    op1=MULT,
+                )
+
+        def second_product(h, mp):
+            tag = "wa%d%d" % (h, mp)
+            acc = psum.tile([P, 2, HALF], F32, name="acc_" + tag, tag=tag)
+            for q in range(2):
+                cols = slice(q * P, (q + 1) * P)
+                nc.tensor.matmul_mx(
+                    out=acc[:, q, :],
+                    lhsT=codes["w1", mp][:, cols].bitcast(FP8X4),
+                    lhsT_scale=scales["w1", mp][:, cols],
+                    rhs=codes["z", h][:].bitcast(FP8X4),
+                    rhs_scale=scales["z", h][:],
+                    start=True,
+                    stop=True,
+                )
+            banks["out", h, mp] = acc
+
+        def finish(h, mp):
+            cols = slice(h * HALF, (h + 1) * HALF)
+            result = keep.tile([P, 2, HALF], F32, name="result%d%d" % (h, mp))
+            nc.vector.tensor_tensor(out=result[:], in0=banks["out", h, mp][:], in1=regs[mp][:, :, cols], op=ADD)
+            rows = slice(mp * 2 * P, (mp + 1) * 2 * P)
+            nc.sync.dma_start(out=out[rows, cols].rearrange("(q p) j -> p q j", p=P), in_=result[:])
+
+        nc.vector.memset(scale_rows[:].bitcast(I32), 0)
+        nc.vector.memset(zero[:], 0.0)
+        nc.scalar.activation(out=zero_bias[:], in_=zero[:], func=SILU)
+        nc.sync.dma_start(offsets[:], offs)
+        nc.gpsimd.dma_start(out=gate[:], in_=gt.rearrange("(p t) o -> p (t o)", t=PACK))
+        load_half("wa", wa, 0)
+        load_scales()
+        load_half("wa", wa, 1)
+        load_words()
+        load_half("wb", wb, 0)
+        load_half("wb", wb, 1)
+        load_half("w1", w1, 0)
+        load_half("w1", w1, 1)
+        load_reg(0)
+        load_reg(1)
+        cast("wa", 0, "vector")
+        gather_scales()
+        quantize("wa", 0)
+        cast("wa", 1, "scalar")
+        deal_scales()
+        quantize("wa", 1)
+        gather_words()
+        first_product("wa", 0)
+        first_product("wa", 1)
+        cast("wb", 0, "vector")
+        silu(0)
+        cast("wb", 1, "scalar")
+        quantize("wb", 0)
+        first_product("wb", 0)
+        silu(1)
+        gated(0)
+        quantize("wb", 1)
+        first_product("wb", 1)
+        cast("z", 0, "scalar")
+        cast("w1", 0, "scalar")
+        gated(1)
+        quantize("z", 0)
+        cast("w1", 1, "scalar")
+        cast("z", 1, "vector")
+        quantize("w1", 0)
+        second_product(0, 0)
+        quantize("z", 1)
+        second_product(1, 0)
+        finish(0, 0)
+        quantize("w1", 1)
+        second_product(0, 1)
+        second_product(1, 1)
+        finish(1, 0)
+        finish(0, 1)
+        finish(1, 1)

@@ -26,6 +26,8 @@ def interleave(nc, engine, dst, src):
     src_walk = src.rearrange("p t (c i) -> p c t i", i=4)
     if engine == "vector":
         nc.vector.tensor_copy(out=dst_walk, in_=src_walk)
+    elif engine == "gpsimd":
+        nc.gpsimd.tensor_scalar(out=dst_walk, in0=src_walk, scalar1=1.0, scalar2=0.0, op0=MULT, op1=ADD)
     else:
         nc.scalar.copy(out=dst_walk, in_=src_walk)
 
@@ -48,9 +50,15 @@ def tile_picked_regmix_silu_p_kernel(
         raw = {}
 
         def load_half(name, src, h):
-            raw[name, h] = keep.tile([P, PACK, HALF], F32, name="raw_%s%d" % (name, h))
+            raw[name, h] = keep.tile([P, PACK, HALF], F32, name="raw_%s%d" % (name, h), align_bytes=64)
             cols = slice(h * HALF, (h + 1) * HALF)
             nc.sync.dma_start(out=raw[name, h][:], in_=src[:, cols].rearrange("(p t) c -> p t c", t=PACK))
+
+        def load_whole(name, src):
+            whole = keep.tile([P, PACK, 2 * HALF], F32, name="raw_%s" % name, align_bytes=64)
+            nc.sync.dma_start(out=whole[:], in_=src.rearrange("(p t) c -> p t c", t=PACK))
+            for h in range(2):
+                raw[name, h] = whole[:, :, h * HALF : (h + 1) * HALF]
 
         def load_scales():
             for q in range(4):
@@ -62,6 +70,13 @@ def tile_picked_regmix_silu_p_kernel(
         def load_words():
             nc.sync.dma_start(out=words[:], in_=x_words[0].rearrange("p n t -> p (n t)").bitcast(I32))
 
+        def load_gate():
+            nc.sync.dma_start(out=gate[:], in_=gt.rearrange("(p t) o -> p (t o)", t=PACK))
+
+        def probe(n, ap):
+            clock = keep.tile([P, 1], ap.dtype, name="clock%d" % n)
+            nc.gpsimd.tensor_copy(out=clock[:], in_=ap)
+
         regs = {}
 
         def load_reg(mp):
@@ -70,12 +85,18 @@ def tile_picked_regmix_silu_p_kernel(
             nc.sync.dma_start(out=regs[mp][:], in_=reg[rows, :].rearrange("(q p) j -> p q j", p=P))
 
         grouped = {}
+        tags = {}
         codes = {}
         scales = {}
 
-        def cast(name, h, engine):
-            grouped[name, h] = keep.tile([P, HALF, PACK], BF16, name="grouped_%s%d" % (name, h), align_bytes=64)
-            interleave(nc, engine, grouped[name, h][:], raw[name, h][:])
+        def cast(name, h, *engines):
+            if (name, h) not in grouped:
+                tag = tags.get((name, h), "grouped_%s%d" % (name, h))
+                grouped[name, h] = keep.tile([P, HALF, PACK], BF16, name="grouped_%s%d" % (name, h), tag=tag, align_bytes=64)[:]
+            share = HALF // len(engines)
+            for n, engine in enumerate(engines):
+                cols = slice(n * share, (n + 1) * share)
+                interleave(nc, engine, grouped[name, h][:, cols, :], raw[name, h][:, :, cols])
 
         def quantize(name, h):
             codes[name, h] = keep.tile([P, HALF], U32, name="codes_%s%d" % (name, h), align_bytes=64)
@@ -83,11 +104,11 @@ def tile_picked_regmix_silu_p_kernel(
             nc.vector.quantize_mx(
                 out=codes[name, h][:].bitcast(FP8X4),
                 scales=scales[name, h][:],
-                in_=grouped[name, h][:].rearrange("p c t -> p (c t)"),
+                in_=grouped[name, h].rearrange("p c t -> p (c t)"),
             )
 
         x_codes = keep.tile([P, S], U32, name="x_codes", align_bytes=64)
-        x_bytes_listed = keep.tile([P, S], U8, name="x_bytes_listed", align_bytes=64)
+        x_bytes_listed = keep.tile([P, S], U8, name="x_bytes_listed", tag="scales_wa0", align_bytes=64)
         x_bytes = keep.tile([P, S], U8, name="x_bytes", align_bytes=64)
 
         def gather_scales():
@@ -126,18 +147,20 @@ def tile_picked_regmix_silu_p_kernel(
         silus = {}
 
         def silu(h):
+            silus[h] = keep.tile([P, PACK, HALF], F32, name="silu%d" % h, tag="raw_wb%d" % h, align_bytes=64)
             for tp in range(2):
-                silus[h, tp] = keep.tile([P, 2, HALF], F32, name="silu%d%d" % (h, tp))
-                nc.scalar.activation(out=silus[h, tp][:], in_=banks["wa", h, tp][:], func=SILU, bias=zero_bias[:])
+                nc.scalar.activation(
+                    out=silus[h][:, 2 * tp : 2 * tp + 2, :], in_=banks["wa", h, tp][:], func=SILU, bias=zero_bias[:]
+                )
 
         def gated(h):
-            raw["z", h] = keep.tile([P, PACK, HALF], BF16, name="raw_z%d" % h)
+            raw["z", h] = keep.tile([P, PACK, HALF], BF16, name="raw_z%d" % h, tag=tags.get(("raw_z", h), "raw_z%d" % h), align_bytes=64)
             for t in range(PACK):
                 nc.vector.scalar_tensor_tensor(
                     out=raw["z", h][:, t, :],
                     in0=banks["wb", h, t // 2][:, t % 2, :],
                     scalar=gate[:, t : t + 1],
-                    in1=silus[h, t // 2][:, t % 2, :],
+                    in1=silus[h][:, t, :],
                     op0=MULT,
                     op1=MULT,
                 )
@@ -169,49 +192,51 @@ def tile_picked_regmix_silu_p_kernel(
         nc.vector.memset(zero[:], 0.0)
         nc.scalar.activation(out=zero_bias[:], in_=zero[:], func=SILU)
         nc.sync.dma_start(offsets[:], offs)
-        nc.gpsimd.dma_start(out=gate[:], in_=gt.rearrange("(p t) o -> p (t o)", t=PACK))
         load_half("wa", wa, 0)
+        load_gate()
         load_scales()
-        load_half("wa", wa, 1)
         load_words()
         load_half("wb", wb, 0)
+        load_half("wa", wa, 1)
         load_half("wb", wb, 1)
-        load_half("w1", w1, 0)
-        load_half("w1", w1, 1)
+        load_whole("w1", w1)
         load_reg(0)
         load_reg(1)
-        cast("wa", 0, "vector")
+        tags["raw_z", 0] = "raw_wa1"
+        tags["z", 0] = "grouped_wb1"
+        tags["z", 1] = "raw_w1"
+        cast("wa", 0, "scalar")
         gather_scales()
-        quantize("wa", 0)
-        cast("wa", 1, "scalar")
         deal_scales()
-        quantize("wa", 1)
+        quantize("wa", 0)
         gather_words()
         first_product("wa", 0)
-        first_product("wa", 1)
-        cast("wb", 0, "vector")
+        cast("wb", 0, "scalar", "vector")
         silu(0)
-        cast("wb", 1, "scalar")
         quantize("wb", 0)
         first_product("wb", 0)
-        silu(1)
+        cast("wa", 1, "vector")
+        quantize("wa", 1)
+        cast("wb", 1, "scalar")
+        first_product("wa", 1)
         gated(0)
         quantize("wb", 1)
         first_product("wb", 1)
-        cast("z", 0, "scalar")
+        silu(1)
+        cast("z", 0, "vector")
         cast("w1", 0, "scalar")
-        gated(1)
         quantize("z", 0)
+        gated(1)
         cast("w1", 1, "scalar")
-        cast("z", 1, "vector")
         quantize("w1", 0)
         second_product(0, 0)
-        quantize("z", 1)
-        second_product(1, 0)
-        finish(0, 0)
+        cast("z", 1, "scalar", "vector")
         quantize("w1", 1)
         second_product(0, 1)
+        quantize("z", 1)
+        second_product(1, 0)
         second_product(1, 1)
-        finish(1, 0)
+        finish(0, 0)
         finish(0, 1)
+        finish(1, 0)
         finish(1, 1)

@@ -99,7 +99,7 @@ def tile_picked_regmix_silu_p_kernel(
                 interleave(nc, engine, grouped[name, h][:, cols, :], raw[name, h][:, :, cols])
 
         def quantize(name, h):
-            codes[name, h] = keep.tile([P, HALF], U32, name="codes_%s%d" % (name, h), align_bytes=64)
+            codes[name, h] = keep.tile([P, HALF], U32, name="codes_%s%d" % (name, h), tag=tags.get(("codes", name, h), "codes_%s%d" % (name, h)), align_bytes=64)
             scales[name, h] = keep.tile([P, HALF], U8, name="scales_%s%d" % (name, h), align_bytes=64)
             nc.vector.quantize_mx(
                 out=codes[name, h][:].bitcast(FP8X4),
@@ -108,7 +108,7 @@ def tile_picked_regmix_silu_p_kernel(
             )
 
         x_codes = keep.tile([P, S], U32, name="x_codes", align_bytes=64)
-        x_bytes_listed = keep.tile([P, S], U8, name="x_bytes_listed", tag="scales_wa0", align_bytes=64)
+        x_bytes_listed = keep.tile([P, S], U8, name="x_bytes_listed", align_bytes=64)
         x_bytes = keep.tile([P, S], U8, name="x_bytes", align_bytes=64)
 
         def gather_scales():
@@ -147,7 +147,7 @@ def tile_picked_regmix_silu_p_kernel(
         silus = {}
 
         def silu(h):
-            silus[h] = keep.tile([P, PACK, HALF], F32, name="silu%d" % h, tag="raw_wb%d" % h, align_bytes=64)
+            silus[h] = keep.tile([P, PACK, HALF], F32, name="silu%d" % h, tag=tags.get(("silu", h), "silu%d" % h), align_bytes=64)
             for tp in range(2):
                 nc.scalar.activation(
                     out=silus[h][:, 2 * tp : 2 * tp + 2, :], in_=banks["wa", h, tp][:], func=SILU, bias=zero_bias[:]
@@ -188,6 +188,28 @@ def tile_picked_regmix_silu_p_kernel(
             rows = slice(mp * 2 * P, (mp + 1) * 2 * P)
             nc.sync.dma_start(out=out[rows, cols].rearrange("(q p) j -> p q j", p=P), in_=result[:])
 
+        def store(h, mp, q0, q1, result):
+            cols = slice(h * HALF, (h + 1) * HALF)
+            rows = slice((2 * mp + q0) * P, (2 * mp + q1) * P)
+            nc.sync.dma_start(out=out[rows, cols].rearrange("(q p) j -> p q j", p=P), in_=result[:])
+
+        def finish_pool(h, mp):
+            cols = slice(h * HALF, (h + 1) * HALF)
+            staged = keep.tile([P, 2, HALF], F32, name="staged", tag="raw_z1", align_bytes=64)
+            nc.scalar.copy(out=staged[:], in_=banks["out", h, mp][:])
+            result = keep.tile([P, 2, HALF], F32, name="result%d%d" % (h, mp))
+            nc.gpsimd.tensor_tensor(out=result[:], in0=staged[:], in1=regs[mp][:, :, cols], op=ADD)
+            store(h, mp, 0, 2, result)
+
+        def finish_split(h, mp):
+            cols = slice(h * HALF, (h + 1) * HALF)
+            for q in range(2):
+                result = keep.tile([P, 1, HALF], F32, name="result%d%d%d" % (h, mp, q))
+                nc.vector.tensor_tensor(
+                    out=result[:], in0=banks["out", h, mp][:, q : q + 1, :], in1=regs[mp][:, q : q + 1, cols], op=ADD
+                )
+                store(h, mp, q, q + 1, result)
+
         nc.vector.memset(scale_rows[:].bitcast(I32), 0)
         nc.vector.memset(zero[:], 0.0)
         nc.scalar.activation(out=zero_bias[:], in_=zero[:], func=SILU)
@@ -199,12 +221,14 @@ def tile_picked_regmix_silu_p_kernel(
         load_half("wb", wb, 0)
         load_half("wa", wa, 1)
         load_half("wb", wb, 1)
-        load_whole("w1", w1)
+        load_half("w1", w1, 0)
+        load_half("w1", w1, 1)
         load_reg(0)
         load_reg(1)
         tags["raw_z", 0] = "raw_wa1"
-        tags["z", 0] = "grouped_wb1"
-        tags["z", 1] = "raw_w1"
+        tags["z", 0] = "raw_wb1"
+        tags["silu", 0] = "raw_wb0"
+        tags["codes", "wa", 0] = "scale_rows"
         cast("wa", 0, "scalar")
         gather_scales()
         deal_scales()
@@ -239,4 +263,4 @@ def tile_picked_regmix_silu_p_kernel(
         finish(0, 0)
         finish(0, 1)
         finish(1, 0)
-        finish(1, 1)
+        finish_split(1, 1)

@@ -19,17 +19,11 @@ SILU = mybir.ActivationFunctionType.Silu
 P = 128
 PACK = 4
 HALF = 256
-
-
-def interleave(nc, engine, dst, src):
-    dst_walk = dst.rearrange("p (c i) t -> p c t i", i=4)
-    src_walk = src.rearrange("p t (c i) -> p c t i", i=4)
-    if engine == "vector":
-        nc.vector.tensor_copy(out=dst_walk, in_=src_walk)
-    elif engine == "gpsimd":
-        nc.gpsimd.tensor_scalar(out=dst_walk, in0=src_walk, scalar1=1.0, scalar2=0.0, op0=MULT, op1=ADD)
-    else:
-        nc.scalar.copy(out=dst_walk, in_=src_walk)
+QUADRANT = 32
+RUN = 4
+ALIGN = 64
+WB_SCALAR_COLUMNS = 128
+Z_SCALAR_COLUMNS = 96
 
 
 def tile_picked_regmix_silu_p_kernel(
@@ -37,127 +31,78 @@ def tile_picked_regmix_silu_p_kernel(
 ):
     nc = tc.nc
     with ExitStack() as ctx:
-        keep = ctx.enter_context(tc.tile_pool(name="keep", bufs=1))
+        sbuf = ctx.enter_context(tc.tile_pool(name="sbuf", bufs=1))
         psum = ctx.enter_context(tc.psum_pool(name="psum", bufs=1))
 
-        offsets = keep.tile([P, S // 16], U16, name="offsets")
-        words = keep.tile([P, T], I32, name="words", align_bytes=64)
-        scale_rows = keep.tile([P, T], U8, name="scale_rows", align_bytes=64)
-        gate = keep.tile([P, PACK], F32, name="gate")
-        zero = keep.tile([P, 1], F32, name="zero")
-        zero_bias = keep.tile([P, 1], F32, name="zero_bias")
+        def new_tile(shape, dtype, name, on=None):
+            return sbuf.tile(shape, dtype, name=name, tag=on or name, align_bytes=ALIGN)
 
-        raw = {}
+        def half(h):
+            return slice(h * HALF, (h + 1) * HALF)
+
+        slots, words_in, codes, scales = {}, {}, {}, {}
+        banks, silus, regs = {}, {}, {}
 
         def load_half(name, src, h):
-            raw[name, h] = keep.tile([P, PACK, HALF], F32, name="raw_%s%d" % (name, h), align_bytes=64)
-            cols = slice(h * HALF, (h + 1) * HALF)
-            nc.sync.dma_start(out=raw[name, h][:], in_=src[:, cols].rearrange("(p t) c -> p t c", t=PACK))
+            slots[name, h] = new_tile([P, PACK, HALF], F32, "slots_%s%d" % (name, h))
+            nc.sync.dma_start(out=slots[name, h][:], in_=src[:, half(h)].rearrange("(p t) c -> p t c", t=PACK))
 
-        def load_whole(name, src):
-            whole = keep.tile([P, PACK, 2 * HALF], F32, name="raw_%s" % name, align_bytes=64)
-            nc.sync.dma_start(out=whole[:], in_=src.rearrange("(p t) c -> p t c", t=PACK))
-            for h in range(2):
-                raw[name, h] = whole[:, :, h * HALF : (h + 1) * HALF]
+        def load_registers(r):
+            regs[r] = new_tile([P, 2, H], F32, "reg%d" % r)
+            nc.sync.dma_start(out=regs[r][:], in_=reg[half(r), :].rearrange("(q p) j -> p q j", p=P))
 
-        def load_scales():
-            for q in range(4):
-                nc.sync.dma_start(
-                    out=scale_rows[32 * q : 32 * q + 4, :].bitcast(I32),
-                    in_=x_scales[0, 4 * q : 4 * q + 4, :].bitcast(I32),
-                )
+        def interleave(name, h, scalar_columns, on=None):
+            words_in[name, h] = new_tile([P, HALF, PACK], BF16, "words_in_%s%d" % (name, h), on)
+            for copy, cols in (
+                (nc.scalar.copy, slice(0, scalar_columns)),
+                (nc.vector.tensor_copy, slice(scalar_columns, HALF)),
+            ):
+                if cols.stop > cols.start:
+                    copy(
+                        out=words_in[name, h][:, cols, :].rearrange("p (c i) t -> p c t i", i=RUN),
+                        in_=slots[name, h][:, :, cols].rearrange("p t (c i) -> p c t i", i=RUN),
+                    )
 
-        def load_words():
-            nc.sync.dma_start(out=words[:], in_=x_words[0].rearrange("p n t -> p (n t)").bitcast(I32))
-
-        def load_gate():
-            nc.sync.dma_start(out=gate[:], in_=gt.rearrange("(p t) o -> p (t o)", t=PACK))
-
-        def probe(n, ap):
-            clock = keep.tile([P, 1], ap.dtype, name="clock%d" % n)
-            nc.gpsimd.tensor_copy(out=clock[:], in_=ap)
-
-        regs = {}
-
-        def load_reg(mp):
-            regs[mp] = keep.tile([P, 2, H], F32, name="reg%d" % mp)
-            rows = slice(mp * 2 * P, (mp + 1) * 2 * P)
-            nc.sync.dma_start(out=regs[mp][:], in_=reg[rows, :].rearrange("(q p) j -> p q j", p=P))
-
-        grouped = {}
-        tags = {}
-        codes = {}
-        scales = {}
-
-        def cast(name, h, *engines):
-            if (name, h) not in grouped:
-                tag = tags.get((name, h), "grouped_%s%d" % (name, h))
-                grouped[name, h] = keep.tile([P, HALF, PACK], BF16, name="grouped_%s%d" % (name, h), tag=tag, align_bytes=64)[:]
-            share = HALF // len(engines)
-            for n, engine in enumerate(engines):
-                cols = slice(n * share, (n + 1) * share)
-                interleave(nc, engine, grouped[name, h][:, cols, :], raw[name, h][:, :, cols])
-
-        def quantize(name, h):
-            codes[name, h] = keep.tile([P, HALF], U32, name="codes_%s%d" % (name, h), tag=tags.get(("codes", name, h), "codes_%s%d" % (name, h)), align_bytes=64)
-            scales[name, h] = keep.tile([P, HALF], U8, name="scales_%s%d" % (name, h), align_bytes=64)
+        def quantize(name, h, on=None):
+            codes[name, h] = new_tile([P, HALF], U32, "codes_%s%d" % (name, h), on)
+            scales[name, h] = new_tile([P, HALF], U8, "scales_%s%d" % (name, h))
             nc.vector.quantize_mx(
                 out=codes[name, h][:].bitcast(FP8X4),
                 scales=scales[name, h][:],
-                in_=grouped[name, h].rearrange("p c t -> p (c t)"),
+                in_=words_in[name, h][:].rearrange("p c t -> p (c t)"),
             )
 
-        x_codes = keep.tile([P, S], U32, name="x_codes", align_bytes=64)
-        x_bytes_listed = keep.tile([P, S], U8, name="x_bytes_listed", align_bytes=64)
-        x_bytes = keep.tile([P, S], U8, name="x_bytes", align_bytes=64)
-
-        def gather_scales():
-            nc.vector.tensor_copy(out=x_bytes_listed[:], in_=scale_rows[:].indirect(offsets[:]))
-
-        def deal_scales():
-            nc.vector.tensor_copy(
-                out=x_bytes[:].rearrange("p (t m) -> p t m", t=PACK),
-                in_=x_bytes_listed[:].rearrange("p (m t) -> p t m", t=PACK),
-            )
-
-        def gather_words():
-            nc.vector.tensor_copy(
-                out=x_codes[:].rearrange("p (t m) -> p m t", t=PACK),
-                in_=words[:].bitcast(U32).indirect(offsets[:]),
-            )
-
-        banks = {}
-
-        def first_product(name, h):
-            for tp in range(2):
-                tag = "%s%d%d" % (name, h, tp)
-                banks[name, h, tp] = psum.tile([P, 2, HALF], F32, name="bank_" + tag, tag=tag)
-                for e in range(2):
-                    cols = slice((2 * tp + e) * P, (2 * tp + e + 1) * P)
-                    nc.tensor.matmul_mx(
-                        out=banks[name, h, tp][:, e, :],
-                        lhsT=x_codes[:, cols].bitcast(FP8X4),
-                        lhsT_scale=x_bytes[:, cols],
-                        rhs=codes[name, h][:].bitcast(FP8X4),
-                        rhs_scale=scales[name, h][:],
-                        start=True,
-                        stop=True,
-                    )
-
-        silus = {}
-
-        def silu(h):
-            silus[h] = keep.tile([P, PACK, HALF], F32, name="silu%d" % h, tag=tags.get(("silu", h), "silu%d" % h), align_bytes=64)
-            for tp in range(2):
-                nc.scalar.activation(
-                    out=silus[h][:, 2 * tp : 2 * tp + 2, :], in_=banks["wa", h, tp][:], func=SILU, bias=zero_bias[:]
+        def product(bank, lhs_codes, lhs_scales, first_column, rhs):
+            for e in range(2):
+                cols = slice(first_column + e * P, first_column + (e + 1) * P)
+                nc.tensor.matmul_mx(
+                    out=bank[:, e, :],
+                    lhsT=lhs_codes[:, cols].bitcast(FP8X4),
+                    lhsT_scale=lhs_scales[:, cols],
+                    rhs=codes[rhs][:].bitcast(FP8X4),
+                    rhs_scale=scales[rhs][:],
+                    start=True,
+                    stop=True,
                 )
 
-        def gated(h):
-            raw["z", h] = keep.tile([P, PACK, HALF], BF16, name="raw_z%d" % h, tag=tags.get(("raw_z", h), "raw_z%d" % h), align_bytes=64)
+        def token_product(name, h):
+            for u in range(2):
+                label = "%s%d%d" % (name, h, u)
+                banks[name, h, u] = psum.tile([P, 2, HALF], F32, name="bank_" + label, tag=label)
+                product(banks[name, h, u], x_codes, x_bytes, 2 * u * P, (name, h))
+
+        def silu(h, on=None):
+            silus[h] = new_tile([P, PACK, HALF], F32, "silu%d" % h, on)
+            for u in range(2):
+                nc.scalar.activation(
+                    out=silus[h][:, 2 * u : 2 * u + 2, :], in_=banks["wa", h, u][:], func=SILU, bias=zero_bias[:]
+                )
+
+        def gate_product(h, on=None):
+            slots["z", h] = new_tile([P, PACK, HALF], BF16, "slots_z%d" % h, on)
             for t in range(PACK):
                 nc.vector.scalar_tensor_tensor(
-                    out=raw["z", h][:, t, :],
+                    out=slots["z", h][:, t, :],
                     in0=banks["wb", h, t // 2][:, t % 2, :],
                     scalar=gate[:, t : t + 1],
                     in1=silus[h][:, t, :],
@@ -165,102 +110,93 @@ def tile_picked_regmix_silu_p_kernel(
                     op1=MULT,
                 )
 
-        def second_product(h, mp):
-            tag = "wa%d%d" % (h, mp)
-            acc = psum.tile([P, 2, HALF], F32, name="acc_" + tag, tag=tag)
-            for q in range(2):
-                cols = slice(q * P, (q + 1) * P)
-                nc.tensor.matmul_mx(
-                    out=acc[:, q, :],
-                    lhsT=codes["w1", mp][:, cols].bitcast(FP8X4),
-                    lhsT_scale=scales["w1", mp][:, cols],
-                    rhs=codes["z", h][:].bitcast(FP8X4),
-                    rhs_scale=scales["z", h][:],
-                    start=True,
-                    stop=True,
-                )
-            banks["out", h, mp] = acc
+        def register_product(h, r):
+            label = "wa%d%d" % (h, r)
+            banks["out", h, r] = psum.tile([P, 2, HALF], F32, name="out_" + label, tag=label)
+            product(banks["out", h, r], codes["w1", r], scales["w1", r], 0, ("z", h))
 
-        def finish(h, mp):
-            cols = slice(h * HALF, (h + 1) * HALF)
-            result = keep.tile([P, 2, HALF], F32, name="result%d%d" % (h, mp))
-            nc.vector.tensor_tensor(out=result[:], in0=banks["out", h, mp][:], in1=regs[mp][:, :, cols], op=ADD)
-            rows = slice(mp * 2 * P, (mp + 1) * 2 * P)
-            nc.sync.dma_start(out=out[rows, cols].rearrange("(q p) j -> p q j", p=P), in_=result[:])
-
-        def store(h, mp, q0, q1, result):
-            cols = slice(h * HALF, (h + 1) * HALF)
-            rows = slice((2 * mp + q0) * P, (2 * mp + q1) * P)
-            nc.sync.dma_start(out=out[rows, cols].rearrange("(q p) j -> p q j", p=P), in_=result[:])
-
-        def finish_pool(h, mp):
-            cols = slice(h * HALF, (h + 1) * HALF)
-            staged = keep.tile([P, 2, HALF], F32, name="staged", tag="raw_z1", align_bytes=64)
-            nc.scalar.copy(out=staged[:], in_=banks["out", h, mp][:])
-            result = keep.tile([P, 2, HALF], F32, name="result%d%d" % (h, mp))
-            nc.gpsimd.tensor_tensor(out=result[:], in0=staged[:], in1=regs[mp][:, :, cols], op=ADD)
-            store(h, mp, 0, 2, result)
-
-        def finish_split(h, mp):
-            cols = slice(h * HALF, (h + 1) * HALF)
-            for q in range(2):
-                result = keep.tile([P, 1, HALF], F32, name="result%d%d%d" % (h, mp, q))
+        def add_and_store(h, r, tiles_at_once, on=None):
+            result = new_tile([P, 2, HALF], F32, "result%d%d" % (h, r), on)
+            for q in range(0, 2, tiles_at_once):
+                tiles = slice(q, q + tiles_at_once)
                 nc.vector.tensor_tensor(
-                    out=result[:], in0=banks["out", h, mp][:, q : q + 1, :], in1=regs[mp][:, q : q + 1, cols], op=ADD
+                    out=result[:, tiles, :], in0=banks["out", h, r][:, tiles, :], in1=regs[r][:, tiles, half(h)], op=ADD
                 )
-                store(h, mp, q, q + 1, result)
+                rows = slice(r * HALF + tiles.start * P, r * HALF + tiles.stop * P)
+                nc.sync.dma_start(out=out[rows, half(h)].rearrange("(q p) j -> p q j", p=P), in_=result[:, tiles, :])
 
-        nc.vector.memset(scale_rows[:].bitcast(I32), 0)
+        offsets = sbuf.tile([P, S // 16], U16, name="offsets")
+        x_table = new_tile([P, T], I32, "x_table")
+        scale_table = new_tile([P, T], U8, "scale_table")
+        gate = new_tile([P, PACK], F32, "gate")
+        zero = new_tile([P, 1], F32, "zero")
+        zero_bias = new_tile([P, 1], F32, "zero_bias")
+        x_codes = new_tile([P, S], U32, "x_codes")
+        x_bytes_listed = new_tile([P, S], U8, "x_bytes_listed")
+        x_bytes = new_tile([P, S], U8, "x_bytes")
+
+        nc.vector.memset(scale_table[:].bitcast(I32), 0)
         nc.vector.memset(zero[:], 0.0)
         nc.scalar.activation(out=zero_bias[:], in_=zero[:], func=SILU)
+
         nc.sync.dma_start(offsets[:], offs)
         load_half("wa", wa, 0)
-        load_gate()
-        load_scales()
-        load_words()
+        nc.sync.dma_start(out=gate[:], in_=gt.rearrange("(p t) o -> p (t o)", t=PACK))
+        for q in range(P // QUADRANT):
+            nc.sync.dma_start(
+                out=scale_table[QUADRANT * q : QUADRANT * q + 4, :].bitcast(I32),
+                in_=x_scales[0, 4 * q : 4 * q + 4, :].bitcast(I32),
+            )
+        nc.sync.dma_start(out=x_table[:], in_=x_words[0].rearrange("p n t -> p (n t)").bitcast(I32))
         load_half("wb", wb, 0)
         load_half("wa", wa, 1)
         load_half("wb", wb, 1)
-        load_half("w1", w1, 0)
-        load_half("w1", w1, 1)
-        load_reg(0)
-        load_reg(1)
-        tags["raw_z", 0] = "raw_wa1"
-        tags["z", 0] = "raw_wb1"
-        tags["silu", 0] = "raw_wb0"
-        tags["codes", "wa", 0] = "scale_rows"
-        cast("wa", 0, "scalar")
-        gather_scales()
-        deal_scales()
-        quantize("wa", 0)
-        gather_words()
-        first_product("wa", 0)
-        cast("wb", 0, "scalar", "vector")
-        silu(0)
+        for r in range(2):
+            load_half("w1", w1, r)
+        for r in range(2):
+            load_registers(r)
+
+        interleave("wa", 0, HALF)
+        nc.vector.tensor_copy(out=x_bytes_listed[:], in_=scale_table[:].indirect(offsets[:]))
+        nc.vector.tensor_copy(
+            out=x_bytes[:].rearrange("p (t m) -> p t m", t=PACK),
+            in_=x_bytes_listed[:].rearrange("p (m t) -> p t m", t=PACK),
+        )
+        quantize("wa", 0, on="scale_table")
+        nc.vector.tensor_copy(
+            out=x_codes[:].rearrange("p (t m) -> p m t", t=PACK),
+            in_=x_table[:].bitcast(U32).indirect(offsets[:]),
+        )
+
+        token_product("wa", 0)
+        interleave("wb", 0, WB_SCALAR_COLUMNS)
+        silu(0, on="slots_wb0")
         quantize("wb", 0)
-        first_product("wb", 0)
-        cast("wa", 1, "vector")
+        token_product("wb", 0)
+        interleave("wa", 1, 0)
         quantize("wa", 1)
-        cast("wb", 1, "scalar")
-        first_product("wa", 1)
-        gated(0)
+        interleave("wb", 1, HALF)
+        token_product("wa", 1)
+        gate_product(0, on="slots_wa1")
         quantize("wb", 1)
-        first_product("wb", 1)
+        token_product("wb", 1)
+
         silu(1)
-        cast("z", 0, "vector")
-        cast("w1", 0, "scalar")
+        interleave("z", 0, 0, on="slots_wb1")
+        interleave("w1", 0, HALF)
         quantize("z", 0)
-        gated(1)
-        cast("w1", 1, "scalar")
+        gate_product(1)
+        interleave("w1", 1, HALF)
         quantize("w1", 0)
-        second_product(0, 0)
-        cast("z", 1, "scalar", "vector")
+        register_product(0, 0)
+        interleave("z", 1, Z_SCALAR_COLUMNS)
         quantize("w1", 1)
-        second_product(0, 1)
+        register_product(0, 1)
         quantize("z", 1)
-        second_product(1, 0)
-        second_product(1, 1)
-        finish(0, 0)
-        finish(0, 1)
-        finish(1, 0)
-        finish_split(1, 1)
+        for r in range(2):
+            register_product(1, r)
+
+        add_and_store(0, 0, 2, on="slots_z1")
+        add_and_store(0, 1, 2)
+        add_and_store(1, 0, 2)
+        add_and_store(1, 1, 1)

@@ -139,9 +139,8 @@ def tile_picked_regmix_silu_p_kernel(
         nc.vector.memset(zero[:], 0.0)
         nc.scalar.activation(out=zero_bias[:], in_=zero[:], func=SILU)
 
-        nc.sync.dma_start(offsets[:], offs)
         load_half("wa", wa, 0)
-        nc.sync.dma_start(out=gate[:], in_=gt.rearrange("(p t) o -> p (t o)", t=PACK))
+        nc.sync.dma_start(offsets[:], offs)
         for q in range(P // QUADRANT):
             nc.sync.dma_start(
                 out=scale_table[QUADRANT * q : QUADRANT * q + 4, :].bitcast(I32),
@@ -149,6 +148,7 @@ def tile_picked_regmix_silu_p_kernel(
             )
         nc.sync.dma_start(out=x_table[:], in_=x_words[0].rearrange("p n t -> p (n t)").bitcast(I32))
         load_half("wb", wb, 0)
+        nc.sync.dma_start(out=gate[:], in_=gt.rearrange("(p t) o -> p (t o)", t=PACK))
         load_half("wa", wa, 1)
         load_half("wb", wb, 1)
         for r in range(2):

from contextlib import ExitStack

import concourse.mybir as mybir

K, T, S, N, H = 512, 2048, 512, 512, 512
FLOPS = 2 * K * S * H * 2 + 2 * S * N * H

F32 = mybir.dt.float32
BF16 = mybir.dt.bfloat16
I32 = mybir.dt.int32
U32 = mybir.dt.uint32
U16 = mybir.dt.uint16
U8 = mybir.dt.uint8
FP8X4 = mybir.dt.float8_e4m3fn_x4
MULT = mybir.AluOpType.mult
ADD = mybir.AluOpType.add
SILU = mybir.ActivationFunctionType.Silu

P = 128
PACK = 4
HALF = 256
QUADRANT = 32
RUN = 4
ALIGN = 64
WB_SCALAR_COLUMNS = 128
Z_SCALAR_COLUMNS = 96


def tile_picked_regmix_silu_p_kernel(
    tc, x_words, x_scales, wa, wb, gt, reg, w1, offs, out
):
    nc = tc.nc
    with ExitStack() as ctx:
        sbuf = ctx.enter_context(tc.tile_pool(name="sbuf", bufs=1))
        psum = ctx.enter_context(tc.psum_pool(name="psum", bufs=1))

        def new_tile(shape, dtype, name, on=None):
            return sbuf.tile(shape, dtype, name=name, tag=on or name, align_bytes=ALIGN)

        def half(h):
            return slice(h * HALF, (h + 1) * HALF)

        slots, words_in, codes, scales = {}, {}, {}, {}
        banks, silus, regs = {}, {}, {}

        def load_half(name, src, h):
            slots[name, h] = new_tile([P, PACK, HALF], F32, "slots_%s%d" % (name, h))
            nc.sync.dma_start(out=slots[name, h][:], in_=src[:, half(h)].rearrange("(p t) c -> p t c", t=PACK))

        def load_registers(r):
            regs[r] = new_tile([P, 2, H], F32, "reg%d" % r)
            nc.sync.dma_start(out=regs[r][:], in_=reg[half(r), :].rearrange("(q p) j -> p q j", p=P))

        def interleave(name, h, scalar_columns, on=None):
            words_in[name, h] = new_tile([P, HALF, PACK], BF16, "words_in_%s%d" % (name, h), on)
            for copy, cols in (
                (nc.scalar.copy, slice(0, scalar_columns)),
                (nc.vector.tensor_copy, slice(scalar_columns, HALF)),
            ):
                if cols.stop > cols.start:
                    copy(
                        out=words_in[name, h][:, cols, :].rearrange("p (c i) t -> p c t i", i=RUN),
                        in_=slots[name, h][:, :, cols].rearrange("p t (c i) -> p c t i", i=RUN),
                    )

        def quantize(name, h, on=None):
            codes[name, h] = new_tile([P, HALF], U32, "codes_%s%d" % (name, h), on)
            scales[name, h] = new_tile([P, HALF], U8, "scales_%s%d" % (name, h))
            nc.vector.quantize_mx(
                out=codes[name, h][:].bitcast(FP8X4),
                scales=scales[name, h][:],
                in_=words_in[name, h][:].rearrange("p c t -> p (c t)"),
            )

        def product(bank, lhs_codes, lhs_scales, first_column, rhs):
            for e in range(2):
                cols = slice(first_column + e * P, first_column + (e + 1) * P)
                nc.tensor.matmul_mx(
                    out=bank[:, e, :],
                    lhsT=lhs_codes[:, cols].bitcast(FP8X4),
                    lhsT_scale=lhs_scales[:, cols],
                    rhs=codes[rhs][:].bitcast(FP8X4),
                    rhs_scale=scales[rhs][:],
                    start=True,
                    stop=True,
                )

        def token_product(name, h):
            for u in range(2):
                label = "%s%d%d" % (name, h, u)
                banks[name, h, u] = psum.tile([P, 2, HALF], F32, name="bank_" + label, tag=label)
                product(banks[name, h, u], x_codes, x_bytes, 2 * u * P, (name, h))

        def silu(h, on=None):
            silus[h] = new_tile([P, PACK, HALF], F32, "silu%d" % h, on)
            for u in range(2):
                nc.scalar.activation(
                    out=silus[h][:, 2 * u : 2 * u + 2, :], in_=banks["wa", h, u][:], func=SILU, bias=zero_bias[:]
                )

        def gate_product(h, on=None):
            slots["z", h] = new_tile([P, PACK, HALF], BF16, "slots_z%d" % h, on)
            for t in range(PACK):
                nc.vector.scalar_tensor_tensor(
                    out=slots["z", h][:, t, :],
                    in0=banks["wb", h, t // 2][:, t % 2, :],
                    scalar=gate[:, t : t + 1],
                    in1=silus[h][:, t, :],
                    op0=MULT,
                    op1=MULT,
                )

        def register_product(h, r):
            label = "wa%d%d" % (h, r)
            banks["out", h, r] = psum.tile([P, 2, HALF], F32, name="out_" + label, tag=label)
            product(banks["out", h, r], codes["w1", r], scales["w1", r], 0, ("z", h))

        def add_and_store(h, r, tiles_at_once, on=None):
            result = new_tile([P, 2, HALF], F32, "result%d%d" % (h, r), on)
            for q in range(0, 2, tiles_at_once):
                tiles = slice(q, q + tiles_at_once)
                nc.vector.tensor_tensor(
                    out=result[:, tiles, :], in0=banks["out", h, r][:, tiles, :], in1=regs[r][:, tiles, half(h)], op=ADD
                )
                rows = slice(r * HALF + tiles.start * P, r * HALF + tiles.stop * P)
                nc.sync.dma_start(out=out[rows, half(h)].rearrange("(q p) j -> p q j", p=P), in_=result[:, tiles, :])

        offsets = sbuf.tile([P, S // 16], U16, name="offsets")
        x_table = new_tile([P, T], I32, "x_table")
        scale_table = new_tile([P, T], U8, "scale_table")
        gate = new_tile([P, PACK], F32, "gate")
        zero = new_tile([P, 1], F32, "zero")
        zero_bias = new_tile([P, 1], F32, "zero_bias")
        x_codes = new_tile([P, S], U32, "x_codes")
        x_bytes_listed = new_tile([P, S], U8, "x_bytes_listed")
        x_bytes = new_tile([P, S], U8, "x_bytes")

        nc.vector.memset(scale_table[:].bitcast(I32), 0)
        nc.vector.memset(zero[:], 0.0)
        nc.scalar.activation(out=zero_bias[:], in_=zero[:], func=SILU)

        load_half("wa", wa, 0)
        nc.sync.dma_start(offsets[:], offs)
        for q in range(P // QUADRANT):
            nc.sync.dma_start(
                out=scale_table[QUADRANT * q : QUADRANT * q + 4, :].bitcast(I32),
                in_=x_scales[0, 4 * q : 4 * q + 4, :].bitcast(I32),
            )
        nc.sync.dma_start(out=x_table[:], in_=x_words[0].rearrange("p n t -> p (n t)").bitcast(I32))
        load_half("wb", wb, 0)
        nc.sync.dma_start(out=gate[:], in_=gt.rearrange("(p t) o -> p (t o)", t=PACK))
        load_half("wa", wa, 1)
        load_half("wb", wb, 1)
        for r in range(2):
            load_half("w1", w1, r)
        for r in range(2):
            load_registers(r)

        interleave("wa", 0, HALF)
        nc.vector.tensor_copy(out=x_bytes_listed[:], in_=scale_table[:].indirect(offsets[:]))
        nc.vector.tensor_copy(
            out=x_bytes[:].rearrange("p (t m) -> p t m", t=PACK),
            in_=x_bytes_listed[:].rearrange("p (m t) -> p t m", t=PACK),
        )
        quantize("wa", 0, on="scale_table")
        nc.vector.tensor_copy(
            out=x_codes[:].rearrange("p (t m) -> p m t", t=PACK),
            in_=x_table[:].bitcast(U32).indirect(offsets[:]),
        )

        token_product("wa", 0)
        interleave("wb", 0, WB_SCALAR_COLUMNS)
        silu(0, on="slots_wb0")
        quantize("wb", 0)
        token_product("wb", 0)
        interleave("wa", 1, 0)
        quantize("wa", 1)
        interleave("wb", 1, HALF)
        token_product("wa", 1)
        gate_product(0, on="slots_wa1")
        quantize("wb", 1)
        token_product("wb", 1)

        silu(1)
        interleave("z", 0, 0, on="slots_wb1")
        interleave("w1", 0, HALF)
        quantize("z", 0)
        gate_product(1)
        interleave("w1", 1, HALF)
        quantize("w1", 0)
        register_product(0, 0)
        interleave("z", 1, Z_SCALAR_COLUMNS)
        quantize("w1", 1)
        register_product(0, 1)
        quantize("z", 1)
        for r in range(2):
            register_product(1, r)

        add_and_store(0, 0, 2, on="slots_z1")
        add_and_store(0, 1, 2)
        add_and_store(1, 0, 2)
        add_and_store(1, 1, 1)
